import numpy as np
import ml_dtypes


def mxq(x, axis, fmt="e4m3"):
    dtype, down = {"e4m3": (ml_dtypes.float8_e4m3fn, 7), "e5m2": (ml_dtypes.float8_e5m2, 14)}[fmt]
    v = np.moveaxis(np.asarray(x, np.float32).astype(ml_dtypes.bfloat16).astype(np.float64), axis, -1)
    blocks = v.reshape(v.shape[:-1] + (-1, 32))
    amax = np.abs(blocks).max(-1, keepdims=True)
    byte = np.maximum(np.where(amax > 0, np.frexp(amax)[1] - 1 + 127, 0) - down, 1)
    scale = np.exp2(byte - 127.0)
    codes = (blocks / scale).astype(np.float32).astype(dtype).astype(np.float64)
    return np.moveaxis((codes * scale).reshape(v.shape), -1, axis)


WIDE = False


def mx_kscale(k):
    if not WIDE:
        return np.ones(k)
    levels = np.array([10, -10, 5, -5, 0])
    if k % 512:
        return np.exp2(np.random.permutation(np.resize(levels, k // 32))).repeat(32)
    a = np.empty((k // 512, 16))
    for p in range(k // 512):
        a[p, :8] = np.random.permutation(np.resize(levels, 8))
        for g in range(8):
            far = levels[np.abs(levels - a[p, g]) >= 10]
            a[p, g + 8] = far[np.random.randint(len(far))]
    return np.exp2(a.ravel()).repeat(32)


def f64(x):
    return np.asarray(x).astype(np.float64)


def striped8(idx):
    return np.concatenate([v.reshape(-1, 16).T for v in idx]).astype(np.uint16)


def unstriped8(offs):
    return np.stack([offs[16 * g:16 * g + 16].T.reshape(-1) for g in range(8)]).astype(np.int64)


E2M1 = np.array([0.0, 0.5, 1.0, 1.5, 2.0, 3.0, 4.0, 6.0, -0.0, -0.5, -1.0, -1.5, -2.0, -3.0, -4.0, -6.0])


def pack_weight(w, fmt):
    k, n = w.shape
    w = f64(np.asarray(w, np.float32).astype(ml_dtypes.bfloat16)).reshape(k // 32, 32, n)
    amax = np.abs(w).max(1)
    if fmt == "e4m3":
        byte = np.frexp(amax)[1] - 1 + 127 - 7
    else:
        mant, ex = np.frexp(amax / 6.0)
        byte = np.where(mant > 0.5, ex, ex - 1) + 127
    byte = np.clip(np.where(amax > 0, byte, 1), 1, 254)
    scaled = (w * np.exp2(127.0 - byte)[:, None, :]).reshape(k, n).astype(np.float32)
    by_word = np.ascontiguousarray(scaled.reshape(k // 512, 128, 4, n).transpose(0, 1, 3, 2))
    if fmt == "e4m3":
        words = by_word.astype(ml_dtypes.float8_e4m3fn).view(np.uint8)
    else:
        c = by_word.astype(ml_dtypes.float4_e2m1fn).view(np.uint8) & 0xF
        words = (c[..., 0::2] | (c[..., 1::2] << 4)).reshape(k // 512, 128, 2 * n)
    return np.ascontiguousarray(words), np.ascontiguousarray(byte.astype(np.uint8).reshape(k // 512, 16, n))


def unpack_weight(words, scales, fmt):
    g, _, n = scales.shape
    words = np.ascontiguousarray(words).reshape(g, 128, n, -1)
    if fmt == "e4m3":
        vals = words.view(ml_dtypes.float8_e4m3fn).astype(np.float64)
    else:
        nib = np.empty((g, 128, n, 4), np.uint8)
        nib[..., 0::2] = words & 0xF
        nib[..., 1::2] = words >> 4
        vals = E2M1[nib]
    vals = vals * np.repeat(np.exp2(scales.astype(np.float64) - 127.0), 8, axis=1)[..., None]
    return vals.transpose(0, 1, 3, 2).reshape(g * 512, n)


K, M, T, S = 1536, 128, 1024, 512


def setup_inputs():
    n = np.random.standard_normal
    s = mx_kscale(K)[:, None]
    w = n((K, M)) / np.sqrt(K) / s
    w4 = pack_weight(w, "e2m1")
    rest = w - unpack_weight(*w4, "e2m1")
    p_r8 = pack_weight(rest, "e4m3")
    return {
        "xT": (n((K, T)) * s).astype(np.float32),
        "w4_words": w4[0],
        "w4_scales": w4[1],
        "r8_words": p_r8[0],
        "r8_scales": p_r8[1],
        "wgt": np.repeat(np.random.uniform(0.5, 2.0, (8, S)), 16, axis=0).astype(np.float32),
        "offs": striped8(np.stack([np.random.permutation(T)[:S] for _ in range(8)])),
    }


def reference(xT, w4_words, w4_scales, r8_words, r8_scales, wgt, offs):
    idx = unstriped8(offs)
    group = np.arange(K) % 512 // 64
    xg = f64(wgt)[np.arange(K) // 4 % 128] * f64(xT)[np.arange(K)[:, None], idx[group]]
    xT_ = mxq(xg, 0, "e4m3")
    w4_ = unpack_weight(w4_words, w4_scales, "e2m1")
    r8_ = unpack_weight(r8_words, r8_scales, "e4m3")
    y = w4_.T @ xT_ + r8_.T @ xT_
    return y

@@ -1,0 +1,149 @@
+from contextlib import ExitStack
+
+import concourse.mybir as mybir
+
+K, M, T, S = 1536, 128, 1024, 512
+FLOPS = 2 * K * M * S * 2
+
+F32 = mybir.dt.float32
+BF16 = mybir.dt.bfloat16
+U8 = mybir.dt.uint8
+U16 = mybir.dt.uint16
+U32 = mybir.dt.uint32
+I32 = mybir.dt.int32
+E4M3 = mybir.dt.float8_e4m3fn_x4
+E2M1 = mybir.dt.float4_e2m1fn_x4
+MULT = mybir.AluOpType.mult
+
+P = 128
+PASSES = K // 512
+HALF = 256
+CHUNK = 128
+
+
+def tile_list_heads_none_kernel(
+    tc, xT, w4_words, w4_scales, r8_words, r8_scales, wgt, offs, out
+):
+    nc = tc.nc
+    with ExitStack() as ctx:
+        keep = ctx.enter_context(tc.tile_pool(name="keep", bufs=1))
+        psum = ctx.enter_context(tc.psum_pool(name="psum", bufs=1))
+
+        lists = keep.tile([P, S // 16], U16, name="lists")
+        weights = [keep.tile([P, HALF], F32, name="weights%d" % h, align_bytes=64) for h in range(2)]
+        w4 = keep.tile([P, PASSES * 2 * M], U8, name="w4", align_bytes=64)
+        r8 = keep.tile([P, PASSES * 4 * M], U8, name="r8", align_bytes=64)
+        w4s = keep.tile([P, PASSES * M], U8, name="w4s", align_bytes=64)
+        r8s = keep.tile([P, PASSES * M], U8, name="r8s", align_bytes=64)
+        tables = [
+            [keep.tile([P, T], F32, name="table%d%d" % (a, i), align_bytes=64) for i in range(4)]
+            for a in range(PASSES)
+        ]
+        picked = [keep.tile([P, 4, S], F32, name="picked%d" % a, align_bytes=64) for a in range(PASSES)]
+        rounded = [keep.tile([P, S, 4], BF16, name="rounded%d" % a, align_bytes=64) for a in range(PASSES)]
+        codes = [keep.tile([P, S], U32, name="codes%d" % a, align_bytes=64) for a in range(PASSES)]
+        scales = [keep.tile([P, S], U8, name="scales%d" % a, align_bytes=64) for a in range(PASSES)]
+        result = keep.tile([M, S], F32, name="result", align_bytes=64)
+        banks = [psum.tile([M, CHUNK], F32, name="bank%d" % c) for c in range(4)]
+
+        rows = xT.rearrange("(a p i) t -> a i p t", p=P, i=4)
+
+        def load_table(a, i):
+            nc.sync.dma_start(out=tables[a][i][:], in_=rows[a, i])
+
+        nc.sync.dma_start(lists[:], offs)
+        nc.sync.dma_start(out=weights[0][:], in_=wgt[:, 0:HALF])
+        load_table(0, 0)
+        nc.sync.dma_start(out=weights[1][:], in_=wgt[:, HALF:S])
+        for i in range(1, 4):
+            load_table(0, i)
+        for i in range(4):
+            load_table(1, i)
+        nc.sync.dma_start(
+            out=w4[:].bitcast(I32).rearrange("p (a w) -> p a w", a=PASSES),
+            in_=w4_words.bitcast(I32).rearrange("a p w -> p a w"),
+        )
+        nc.sync.dma_start(
+            out=r8[:].bitcast(I32).rearrange("p (a w) -> p a w", a=PASSES),
+            in_=r8_words.bitcast(I32).rearrange("a p n o -> p a (n o)"),
+        )
+        for tile, hbm in ((w4s, w4_scales), (r8s, r8_scales)):
+            nc.vector.memset(tile[:].bitcast(I32), 0)
+            for q in range(4):
+                nc.sync.dma_start(
+                    out=tile[32 * q : 32 * q + 4, :].bitcast(I32).rearrange("p (a w) -> p a w", a=PASSES),
+                    in_=hbm[:, 4 * q : 4 * q + 4, :].bitcast(I32).rearrange("a q w -> q a w"),
+                )
+        for i in range(4):
+            load_table(2, i)
+
+        def pick(a, i, lo, hi):
+            h = lo // HALF
+            nc.vector.tensor_tensor(
+                picked[a][:, i, lo:hi],
+                tables[a][i][:].indirect(lists[:, lo // 16 : hi // 16]),
+                weights[h][:, lo - h * HALF : hi - h * HALF],
+                MULT,
+            )
+
+        def interleave(a, i, lo, hi):
+            nc.scalar.copy(
+                out=rounded[a][:, lo:hi, i : i + 2],
+                in_=picked[a][:, i : i + 2, lo:hi].rearrange("p i c -> p c i"),
+            )
+
+        def quantize(a, lo, hi):
+            nc.vector.quantize_mx(
+                out=codes[a][:, lo:hi].bitcast(E4M3),
+                scales=scales[a][:, lo:hi],
+                in_=rounded[a][:, lo:hi, :].rearrange("p c i -> p (c i)"),
+            )
+
+        def multiply(a, c):
+            cols = slice(c * CHUNK, (c + 1) * CHUNK)
+            nc.tensor.matmul_mx(
+                out=banks[c][:],
+                lhsT=w4[:, a * 2 * M : (a + 1) * 2 * M].bitcast(E2M1),
+                lhsT_scale=w4s[:, a * M : (a + 1) * M],
+                rhs=codes[a][:, cols].bitcast(E4M3),
+                rhs_scale=scales[a][:, cols],
+                start=(a == 0),
+                stop=False,
+            )
+            nc.tensor.matmul_mx(
+                out=banks[c][:],
+                lhsT=r8[:, a * 4 * M : (a + 1) * 4 * M].bitcast(E4M3),
+                lhsT_scale=r8s[:, a * M : (a + 1) * M],
+                rhs=codes[a][:, cols].bitcast(E4M3),
+                rhs_scale=scales[a][:, cols],
+                start=False,
+                stop=(a == PASSES - 1),
+            )
+
+        for a in range(PASSES):
+            for i in range(4):
+                if (a, i) != (2, 3):
+                    for lo in (0, HALF):
+                        pick(a, i, lo, lo + HALF)
+                if i == 1:
+                    interleave(a, 0, 0, S)
+                    if a > 0:
+                        quantize(a - 1, 0, S)
+                        for c in range(4):
+                            multiply(a - 1, c)
+                if i == 3 and a < 2:
+                    interleave(a, 2, 0, S)
+
+        for c in range(4):
+            lo, hi = c * CHUNK, (c + 1) * CHUNK
+            pick(2, 3, lo, hi)
+            interleave(2, 2, lo, hi)
+        for c in range(4):
+            lo, hi = c * CHUNK, (c + 1) * CHUNK
+            quantize(2, lo, hi)
+            multiply(2, c)
+            if c == 3:
+                nc.vector.tensor_copy(out=result[:, lo:hi], in_=banks[c][:])
+            else:
+                nc.scalar.copy(out=result[:, lo:hi], in_=banks[c][:])
+            nc.sync.dma_start(out=out[:, lo:hi], in_=result[:, lo:hi])

@@ -30,7 +30,7 @@ def tile_list_heads_none_kernel(
         psum = ctx.enter_context(tc.psum_pool(name="psum", bufs=1))
 
         lists = keep.tile([P, S // 16], U16, name="lists")
-        weights = [keep.tile([P, HALF], F32, name="weights%d" % h, align_bytes=64) for h in range(2)]
+        weights = keep.tile([P, S], F32, name="weights", align_bytes=64)
         w4 = keep.tile([P, PASSES * 2 * M], U8, name="w4", align_bytes=64)
         r8 = keep.tile([P, PASSES * 4 * M], U8, name="r8", align_bytes=64)
         w4s = keep.tile([P, PASSES * M], U8, name="w4s", align_bytes=64)
@@ -52,13 +52,14 @@ def tile_list_heads_none_kernel(
             nc.sync.dma_start(out=tables[a][i][:], in_=rows[a, i])
 
         nc.sync.dma_start(lists[:], offs)
-        nc.sync.dma_start(out=weights[0][:], in_=wgt[:, 0:HALF])
+        nc.sync.dma_start(out=weights[:, 0:HALF], in_=wgt[:, 0:HALF])
         load_table(0, 0)
-        nc.sync.dma_start(out=weights[1][:], in_=wgt[:, HALF:S])
+        nc.sync.dma_start(out=weights[:, HALF:S], in_=wgt[:, HALF:S])
         for i in range(1, 4):
             load_table(0, i)
-        for i in range(4):
-            load_table(1, i)
+        for a in range(1, PASSES):
+            for i in range(4):
+                load_table(a, i)
         nc.sync.dma_start(
             out=w4[:].bitcast(I32).rearrange("p (a w) -> p a w", a=PASSES),
             in_=w4_words.bitcast(I32).rearrange("a p w -> p a w"),
@@ -74,15 +75,12 @@ def tile_list_heads_none_kernel(
                     out=tile[32 * q : 32 * q + 4, :].bitcast(I32).rearrange("p (a w) -> p a w", a=PASSES),
                     in_=hbm[:, 4 * q : 4 * q + 4, :].bitcast(I32).rearrange("a q w -> q a w"),
                 )
-        for i in range(4):
-            load_table(2, i)
 
         def pick(a, i, lo, hi):
-            h = lo // HALF
             nc.vector.tensor_tensor(
                 picked[a][:, i, lo:hi],
                 tables[a][i][:].indirect(lists[:, lo // 16 : hi // 16]),
-                weights[h][:, lo - h * HALF : hi - h * HALF],
+                weights[:, lo:hi],
                 MULT,
             )
 
@@ -120,27 +118,32 @@ def tile_list_heads_none_kernel(
                 stop=(a == PASSES - 1),
             )
 
-        for a in range(PASSES):
+        for a in range(2):
             for i in range(4):
-                if (a, i) != (2, 3):
-                    for lo in (0, HALF):
-                        pick(a, i, lo, lo + HALF)
-                if i == 1:
-                    interleave(a, 0, 0, S)
-                    if a > 0:
-                        quantize(a - 1, 0, S)
-                        for c in range(4):
-                            multiply(a - 1, c)
-                if i == 3 and a < 2:
-                    interleave(a, 2, 0, S)
+                for lo in (0, HALF):
+                    pick(a, i, lo, lo + HALF)
+                    if i % 2 == 1:
+                        interleave(a, i - 1, lo, lo + HALF)
+            for lo in (0, HALF):
+                quantize(a, lo, lo + HALF)
+            for c in range(4):
+                multiply(a, c)
 
+        EDGE = S - CHUNK
+        for i in range(4):
+            pick(2, i, 0, EDGE)
+            if i % 2 == 1:
+                interleave(2, i - 1, 0, HALF)
+                interleave(2, i - 1, HALF, EDGE)
+        for i in range(4):
+            pick(2, i, EDGE, S)
+            if i % 2 == 1:
+                interleave(2, i - 1, EDGE, S)
+        quantize(2, 0, HALF)
+        quantize(2, HALF, EDGE)
+        quantize(2, EDGE, S)
         for c in range(4):
             lo, hi = c * CHUNK, (c + 1) * CHUNK
-            pick(2, 3, lo, hi)
-            interleave(2, 2, lo, hi)
-        for c in range(4):
-            lo, hi = c * CHUNK, (c + 1) * CHUNK
-            quantize(2, lo, hi)
             multiply(2, c)
             if c == 3:
                 nc.vector.tensor_copy(out=result[:, lo:hi], in_=banks[c][:])

@@ -51,15 +51,23 @@ def tile_list_heads_none_kernel(
         def load_table(a, i):
             nc.sync.dma_start(out=tables[a][i][:], in_=rows[a, i])
 
+        for tile, hbm in ((w4s, w4_scales), (r8s, r8_scales)):
+            nc.vector.memset(tile[:].bitcast(I32), 0)
+            for q in range(4):
+                nc.gpsimd.dma_start(
+                    out=tile[32 * q : 32 * q + 4, :].bitcast(I32).rearrange("p (a w) -> p a w", a=PASSES),
+                    in_=hbm[:, 4 * q : 4 * q + 4, :].bitcast(I32).rearrange("a q w -> q a w"),
+                )
         nc.sync.dma_start(lists[:], offs)
         nc.sync.dma_start(out=weights[:, 0:HALF], in_=wgt[:, 0:HALF])
         load_table(0, 0)
         nc.sync.dma_start(out=weights[:, HALF:S], in_=wgt[:, HALF:S])
         for i in range(1, 4):
             load_table(0, i)
-        for a in range(1, PASSES):
-            for i in range(4):
-                load_table(a, i)
+        for i in range(4):
+            load_table(1, i)
+        for i in range(4):
+            load_table(2, i)
         nc.sync.dma_start(
             out=w4[:].bitcast(I32).rearrange("p (a w) -> p a w", a=PASSES),
             in_=w4_words.bitcast(I32).rearrange("a p w -> p a w"),
@@ -68,13 +76,6 @@ def tile_list_heads_none_kernel(
             out=r8[:].bitcast(I32).rearrange("p (a w) -> p a w", a=PASSES),
             in_=r8_words.bitcast(I32).rearrange("a p n o -> p a (n o)"),
         )
-        for tile, hbm in ((w4s, w4_scales), (r8s, r8_scales)):
-            nc.vector.memset(tile[:].bitcast(I32), 0)
-            for q in range(4):
-                nc.sync.dma_start(
-                    out=tile[32 * q : 32 * q + 4, :].bitcast(I32).rearrange("p (a w) -> p a w", a=PASSES),
-                    in_=hbm[:, 4 * q : 4 * q + 4, :].bitcast(I32).rearrange("a q w -> q a w"),
-                )
 
         def pick(a, i, lo, hi):
             nc.vector.tensor_tensor(
@@ -84,10 +85,10 @@ def tile_list_heads_none_kernel(
                 MULT,
             )
 
-        def interleave(a, i, lo, hi):
-            nc.scalar.copy(
-                out=rounded[a][:, lo:hi, i : i + 2],
-                in_=picked[a][:, i : i + 2, lo:hi].rearrange("p i c -> p c i"),
+        def interleave(copy, a, lo, hi):
+            copy(
+                out=rounded[a][:, lo:hi, :],
+                in_=picked[a][:, :, lo:hi].rearrange("p i c -> p c i"),
             )
 
         def quantize(a, lo, hi):
@@ -122,27 +123,26 @@ def tile_list_heads_none_kernel(
             for i in range(4):
                 for lo in (0, HALF):
                     pick(a, i, lo, lo + HALF)
-                    if i % 2 == 1:
-                        interleave(a, i - 1, lo, lo + HALF)
+                    if i == 3:
+                        interleave(nc.scalar.copy, a, lo, lo + CHUNK)
+                        interleave(nc.scalar.copy, a, lo + CHUNK, lo + HALF)
             for lo in (0, HALF):
                 quantize(a, lo, lo + HALF)
             for c in range(4):
                 multiply(a, c)
 
-        EDGE = S - CHUNK
         for i in range(4):
-            pick(2, i, 0, EDGE)
-            if i % 2 == 1:
-                interleave(2, i - 1, 0, HALF)
-                interleave(2, i - 1, HALF, EDGE)
+            pick(2, i, 0, HALF)
+        interleave(nc.scalar.copy, 2, 0, CHUNK)
+        interleave(nc.scalar.copy, 2, CHUNK, HALF)
         for i in range(4):
-            pick(2, i, EDGE, S)
-            if i % 2 == 1:
-                interleave(2, i - 1, EDGE, S)
+            pick(2, i, HALF, S)
+        interleave(nc.scalar.copy, 2, HALF, HALF + CHUNK)
+        interleave(nc.vector.tensor_copy, 2, HALF + CHUNK, S)
         quantize(2, 0, HALF)
-        quantize(2, HALF, EDGE)
-        quantize(2, EDGE, S)
-        for c in range(4):
+        quantize(2, HALF + CHUNK, S)
+        quantize(2, HALF, HALF + CHUNK)
+        for c in (0, 1, 3, 2):
             lo, hi = c * CHUNK, (c + 1) * CHUNK
             multiply(2, c)
             if c == 3:

@@ -85,10 +85,10 @@ def tile_list_heads_none_kernel(
                 MULT,
             )
 
-        def interleave(copy, a, lo, hi):
+        def interleave(copy, a, slots, lo, hi):
             copy(
-                out=rounded[a][:, lo:hi, :],
-                in_=picked[a][:, :, lo:hi].rearrange("p i c -> p c i"),
+                out=rounded[a][:, lo:hi, slots],
+                in_=picked[a][:, slots, lo:hi].rearrange("p i c -> p c i"),
             )
 
         def quantize(a, lo, hi):
@@ -124,26 +124,25 @@ def tile_list_heads_none_kernel(
                 for lo in (0, HALF):
                     pick(a, i, lo, lo + HALF)
                     if i == 3:
-                        interleave(nc.scalar.copy, a, lo, lo + CHUNK)
-                        interleave(nc.scalar.copy, a, lo + CHUNK, lo + HALF)
+                        interleave(nc.scalar.copy, a, slice(0, 4), lo, lo + CHUNK)
+                        interleave(nc.scalar.copy, a, slice(0, 4), lo + CHUNK, lo + HALF)
             for lo in (0, HALF):
                 quantize(a, lo, lo + HALF)
             for c in range(4):
                 multiply(a, c)
 
-        for i in range(4):
-            pick(2, i, 0, HALF)
-        interleave(nc.scalar.copy, 2, 0, CHUNK)
-        interleave(nc.scalar.copy, 2, CHUNK, HALF)
-        for i in range(4):
-            pick(2, i, HALF, S)
-        interleave(nc.scalar.copy, 2, HALF, HALF + CHUNK)
-        interleave(nc.vector.tensor_copy, 2, HALF + CHUNK, S)
-        quantize(2, 0, HALF)
-        quantize(2, HALF + CHUNK, S)
-        quantize(2, HALF, HALF + CHUNK)
-        for c in (0, 1, 3, 2):
+        for i in range(3):
+            for lo in (0, HALF):
+                pick(2, i, lo, lo + HALF)
+                if i == 1:
+                    interleave(nc.scalar.copy, 2, slice(0, 2), lo, lo + HALF)
+        for c in range(4):
             lo, hi = c * CHUNK, (c + 1) * CHUNK
+            pick(2, 3, lo, hi)
+            interleave(nc.vector.tensor_copy if c == 3 else nc.scalar.copy, 2, slice(2, 4), lo, hi)
+        for c in range(4):
+            lo, hi = c * CHUNK, (c + 1) * CHUNK
+            quantize(2, lo, hi)
             multiply(2, c)
             if c == 3:
                 nc.vector.tensor_copy(out=result[:, lo:hi], in_=banks[c][:])

from contextlib import ExitStack

import concourse.mybir as mybir

K, M, T, S = 1536, 128, 1024, 512
FLOPS = 2 * K * M * S * 2

F32 = mybir.dt.float32
BF16 = mybir.dt.bfloat16
U8 = mybir.dt.uint8
U16 = mybir.dt.uint16
U32 = mybir.dt.uint32
I32 = mybir.dt.int32
E4M3 = mybir.dt.float8_e4m3fn_x4
E2M1 = mybir.dt.float4_e2m1fn_x4
MULT = mybir.AluOpType.mult

P = 128
PASSES = K // 512
HALF = 256
CHUNK = 128


def tile_list_heads_none_kernel(
    tc, xT, w4_words, w4_scales, r8_words, r8_scales, wgt, offs, out
):
    nc = tc.nc
    with ExitStack() as ctx:
        keep = ctx.enter_context(tc.tile_pool(name="keep", bufs=1))
        psum = ctx.enter_context(tc.psum_pool(name="psum", bufs=1))

        lists = keep.tile([P, S // 16], U16, name="lists")
        weights = keep.tile([P, S], F32, name="weights", align_bytes=64)
        w4 = keep.tile([P, PASSES * 2 * M], U8, name="w4", align_bytes=64)
        r8 = keep.tile([P, PASSES * 4 * M], U8, name="r8", align_bytes=64)
        w4s = keep.tile([P, PASSES * M], U8, name="w4s", align_bytes=64)
        r8s = keep.tile([P, PASSES * M], U8, name="r8s", align_bytes=64)
        tables = [
            [keep.tile([P, T], F32, name="table%d%d" % (a, i), align_bytes=64) for i in range(4)]
            for a in range(PASSES)
        ]
        picked = [keep.tile([P, 4, S], F32, name="picked%d" % a, align_bytes=64) for a in range(PASSES)]
        rounded = [keep.tile([P, S, 4], BF16, name="rounded%d" % a, align_bytes=64) for a in range(PASSES)]
        codes = [keep.tile([P, S], U32, name="codes%d" % a, align_bytes=64) for a in range(PASSES)]
        scales = [keep.tile([P, S], U8, name="scales%d" % a, align_bytes=64) for a in range(PASSES)]
        result = keep.tile([M, S], F32, name="result", align_bytes=64)
        banks = [psum.tile([M, CHUNK], F32, name="bank%d" % c) for c in range(4)]

        rows = xT.rearrange("(a p i) t -> a i p t", p=P, i=4)

        def load_table(a, i):
            nc.sync.dma_start(out=tables[a][i][:], in_=rows[a, i])

        for tile, hbm in ((w4s, w4_scales), (r8s, r8_scales)):
            nc.vector.memset(tile[:].bitcast(I32), 0)
            for q in range(4):
                nc.gpsimd.dma_start(
                    out=tile[32 * q : 32 * q + 4, :].bitcast(I32).rearrange("p (a w) -> p a w", a=PASSES),
                    in_=hbm[:, 4 * q : 4 * q + 4, :].bitcast(I32).rearrange("a q w -> q a w"),
                )
        nc.sync.dma_start(lists[:], offs)
        nc.sync.dma_start(out=weights[:, 0:HALF], in_=wgt[:, 0:HALF])
        load_table(0, 0)
        nc.sync.dma_start(out=weights[:, HALF:S], in_=wgt[:, HALF:S])
        for i in range(1, 4):
            load_table(0, i)
        for i in range(4):
            load_table(1, i)
        for i in range(4):
            load_table(2, i)
        nc.sync.dma_start(
            out=w4[:].bitcast(I32).rearrange("p (a w) -> p a w", a=PASSES),
            in_=w4_words.bitcast(I32).rearrange("a p w -> p a w"),
        )
        nc.sync.dma_start(
            out=r8[:].bitcast(I32).rearrange("p (a w) -> p a w", a=PASSES),
            in_=r8_words.bitcast(I32).rearrange("a p n o -> p a (n o)"),
        )

        def pick(a, i, lo, hi):
            nc.vector.tensor_tensor(
                picked[a][:, i, lo:hi],
                tables[a][i][:].indirect(lists[:, lo // 16 : hi // 16]),
                weights[:, lo:hi],
                MULT,
            )

        def interleave(copy, a, slots, lo, hi):
            copy(
                out=rounded[a][:, lo:hi, slots],
                in_=picked[a][:, slots, lo:hi].rearrange("p i c -> p c i"),
            )

        def quantize(a, lo, hi):
            nc.vector.quantize_mx(
                out=codes[a][:, lo:hi].bitcast(E4M3),
                scales=scales[a][:, lo:hi],
                in_=rounded[a][:, lo:hi, :].rearrange("p c i -> p (c i)"),
            )

        def multiply(a, c):
            cols = slice(c * CHUNK, (c + 1) * CHUNK)
            nc.tensor.matmul_mx(
                out=banks[c][:],
                lhsT=w4[:, a * 2 * M : (a + 1) * 2 * M].bitcast(E2M1),
                lhsT_scale=w4s[:, a * M : (a + 1) * M],
                rhs=codes[a][:, cols].bitcast(E4M3),
                rhs_scale=scales[a][:, cols],
                start=(a == 0),
                stop=False,
            )
            nc.tensor.matmul_mx(
                out=banks[c][:],
                lhsT=r8[:, a * 4 * M : (a + 1) * 4 * M].bitcast(E4M3),
                lhsT_scale=r8s[:, a * M : (a + 1) * M],
                rhs=codes[a][:, cols].bitcast(E4M3),
                rhs_scale=scales[a][:, cols],
                start=False,
                stop=(a == PASSES - 1),
            )

        for a in range(2):
            for i in range(4):
                for lo in (0, HALF):
                    pick(a, i, lo, lo + HALF)
                    if i == 3:
                        interleave(nc.scalar.copy, a, slice(0, 4), lo, lo + CHUNK)
                        interleave(nc.scalar.copy, a, slice(0, 4), lo + CHUNK, lo + HALF)
            for lo in (0, HALF):
                quantize(a, lo, lo + HALF)
            for c in range(4):
                multiply(a, c)

        for i in range(3):
            for lo in (0, HALF):
                pick(2, i, lo, lo + HALF)
                if i == 1:
                    interleave(nc.scalar.copy, 2, slice(0, 2), lo, lo + HALF)
        for c in range(4):
            lo, hi = c * CHUNK, (c + 1) * CHUNK
            pick(2, 3, lo, hi)
            interleave(nc.vector.tensor_copy if c == 3 else nc.scalar.copy, 2, slice(2, 4), lo, hi)
        for c in range(4):
            lo, hi = c * CHUNK, (c + 1) * CHUNK
            quantize(2, lo, hi)
            multiply(2, c)
            if c == 3:
                nc.vector.tensor_copy(out=result[:, lo:hi], in_=banks[c][:])
            else:
                nc.scalar.copy(out=result[:, lo:hi], in_=banks[c][:])
            nc.sync.dma_start(out=out[:, lo:hi], in_=result[:, lo:hi])
